import numpy as np
import ml_dtypes

BF16 = ml_dtypes.bfloat16


def bf(x):
    return np.asarray(x, np.float32).astype(BF16)


def f32(x):
    return np.asarray(x, np.float32)


def f64(x):
    return np.asarray(x).astype(np.float64)


def striped(idx):
    return np.tile(idx.reshape(-1, 16).T, (8, 1))


S, K, M, N, H = 1024, 128, 512, 768, 256


def sigmoid(v):
    return 1.0 / (1.0 + np.exp(-v))


def setup_inputs():
    return {"table": bf(np.random.standard_normal((S, K))), "w": bf(np.random.standard_normal((K, M)) / np.sqrt(K)), "offs": striped(np.random.permutation(np.tile(np.arange(S), 2))[:N])}


def reference(table, w, offs):
    idx = offs[:16].T.reshape(-1)
    x = f64(table)[idx].T
    y = f64(w).T @ x
    return y[:H] * sigmoid(y[H:])

import concourse.mybir as mybir
from concourse.masks import make_identity

BF16 = mybir.dt.bfloat16
F32 = mybir.dt.float32
U16 = mybir.dt.uint16

P = 128
WORDS = 1024
TOKENS = 768
GATED = 256
LOADS = (1, 2, 2, 2, 1)
PIECES = (384, 256, 128)
BANKS = 8
WARM = 10
FLOPS = 2 * P * (2 * GATED) * TOKENS


def tile_gather_matmul_kernel(tc, table, w, offs, out):
    nc = tc.nc
    with (
        tc.tile_pool(name="held", bufs=1) as held,
        tc.tile_pool(name="work", bufs=len(PIECES) * GATED // P) as work,
    ):
        identity = held.tile([P, P], BF16, name="identity")
        make_identity(nc, identity[:])

        table_blocks = table.rearrange("(a p) k -> p a k", p=P)
        queues = (nc.sync, nc.scalar)
        rows = []
        block = 0
        for g, blocks in enumerate(LOADS):
            rows.append(held.tile([P, blocks, P], BF16, name="rows%d" % g))
            queues[g % 2].dma_start(rows[g][:], table_blocks[:, block : block + blocks, :])
            block += blocks
        offsets = held.tile([P, TOKENS // 16], U16, name="offsets")
        nc.sync.dma_start(offsets[:], offs)
        gate_weights = held.tile([P, GATED], BF16, name="gate_weights")
        nc.scalar.dma_start(gate_weights[:], w[:, GATED : 2 * GATED])
        value_weights = held.tile([P, GATED], BF16, name="value_weights")
        nc.scalar.dma_start(value_weights[:], w[:, 0:GATED])

        words = held.tile([P, WORDS], BF16, name="words")
        with tc.psum_pool(name="flip", bufs=len(LOADS)) as flip:
            idle = flip.tile([P, P], F32, name="idle", bufs=1)
            for i in range(WARM):
                nc.tensor.matmul(idle[:], identity[:], identity[:], start=True, stop=True)
            block = 0
            for g, blocks in enumerate(LOADS):
                flipped = flip.tile([P, blocks * P], BF16, name="flipped")
                for a in range(blocks):
                    nc.tensor.transpose(flipped[:, a * P : (a + 1) * P], rows[g][:, a, :], identity[:])
                nc.vector.tensor_copy(words[:, block * P : (block + blocks) * P], flipped[:])
                block += blocks

        with tc.psum_pool(name="sums", bufs=BANKS // 2) as sums:
            first = 0
            for size in PIECES:
                piece = offsets[:, first // 16 : (first + size) // 16]
                for h in range(GATED // P):
                    gate = sums.tile([P, size], F32, name="gate")
                    nc.tensor.matmul(gate[:], gate_weights[:, h * P : (h + 1) * P], words[:].indirect(piece), start=True, stop=True)
                    opening = work.tile([P, size], F32, name="opening")
                    nc.scalar.activation(opening[:], gate[:], mybir.ActivationFunctionType.Sigmoid)
                    value = sums.tile([P, size], F32, name="value")
                    nc.tensor.matmul(value[:], value_weights[:, h * P : (h + 1) * P], words[:].indirect(piece), start=True, stop=True)
                    gated = work.tile([P, size], F32, name="gated")
                    nc.vector.tensor_tensor(gated[:], value[:], opening[:], mybir.AluOpType.mult)
                    nc.sync.dma_start(out[h * P : (h + 1) * P, first : first + size], gated[:])
                first += size
